import numpy as np
import ml_dtypes


def mxq(x, axis, fmt="e4m3"):
    dtype, down = {"e4m3": (ml_dtypes.float8_e4m3fn, 7), "e5m2": (ml_dtypes.float8_e5m2, 14)}[fmt]
    v = np.moveaxis(np.asarray(x, np.float32).astype(ml_dtypes.bfloat16).astype(np.float64), axis, -1)
    blocks = v.reshape(v.shape[:-1] + (-1, 32))
    amax = np.abs(blocks).max(-1, keepdims=True)
    byte = np.maximum(np.where(amax > 0, np.frexp(amax)[1] - 1 + 127, 0) - down, 1)
    scale = np.exp2(byte - 127.0)
    codes = (blocks / scale).astype(np.float32).astype(dtype).astype(np.float64)
    return np.moveaxis((codes * scale).reshape(v.shape), -1, axis)


WIDE = False


def mx_kscale(k):
    if not WIDE:
        return np.ones(k)
    levels = np.array([10, -10, 5, -5, 0])
    if k % 512:
        return np.exp2(np.random.permutation(np.resize(levels, k // 32))).repeat(32)
    a = np.empty((k // 512, 16))
    for p in range(k // 512):
        a[p, :8] = np.random.permutation(np.resize(levels, 8))
        for g in range(8):
            far = levels[np.abs(levels - a[p, g]) >= 10]
            a[p, g + 8] = far[np.random.randint(len(far))]
    return np.exp2(a.ravel()).repeat(32)


def f64(x):
    return np.asarray(x).astype(np.float64)


def striped(idx):
    return np.tile(idx.reshape(-1, 16).T, (8, 1)).astype(np.uint16)


def unstriped(offs):
    return offs[:16].T.reshape(-1).astype(np.int64)


def pack_weight(w):
    k, n = w.shape
    w = f64(np.asarray(w, np.float32).astype(ml_dtypes.bfloat16)).reshape(k // 32, 32, n)
    amax = np.abs(w).max(1)
    byte = np.clip(np.where(amax > 0, np.frexp(amax)[1] - 1 + 127 - 7, 1), 1, 254)
    scaled = (w * np.exp2(127.0 - byte)[:, None, :]).reshape(k, n).astype(np.float32)
    words = np.ascontiguousarray(scaled.reshape(k // 512, 128, 4, n).transpose(0, 1, 3, 2)).astype(ml_dtypes.float8_e4m3fn).view(np.uint8)
    return words, np.ascontiguousarray(byte.astype(np.uint8).reshape(k // 512, 16, n))


def unpack_weight(words, scales):
    g, p, n, _ = words.shape
    vals = np.ascontiguousarray(words).view(ml_dtypes.float8_e4m3fn).astype(np.float64) * np.repeat(np.exp2(scales.astype(np.float64) - 127.0), 8, axis=1)[..., None]
    return vals.transpose(0, 1, 3, 2).reshape(g * 512, n)


E2M1 = np.array([0.0, 0.5, 1.0, 1.5, 2.0, 3.0, 4.0, 6.0, -0.0, -0.5, -1.0, -1.5, -2.0, -3.0, -4.0, -6.0])


def pack_fp4(w):
    k, n = w.shape
    w = f64(np.asarray(w, np.float32).astype(ml_dtypes.bfloat16)).reshape(k // 32, 32, n)
    amax = np.abs(w).max(1)
    mant, ex = np.frexp(amax / 6.0)
    byte = np.clip(np.where(amax > 0, np.where(mant > 0.5, ex, ex - 1) + 127, 1), 1, 254)
    scaled = (w * np.exp2(127.0 - byte)[:, None, :]).reshape(k, n).astype(np.float32)
    c = np.ascontiguousarray(scaled.reshape(k // 512, 128, 4, n).transpose(0, 1, 3, 2)).astype(ml_dtypes.float4_e2m1fn).view(np.uint8) & 0xF
    words = (c[..., 0::2] | (c[..., 1::2] << 4)).reshape(k // 512, 128, 2 * n)
    return np.ascontiguousarray(words), np.ascontiguousarray(byte.astype(np.uint8).reshape(k // 512, 16, n))


def unpack_fp4(words, scales):
    g, _, n = scales.shape
    words = np.ascontiguousarray(words).reshape(g, 128, n, 2)
    nib = np.empty((g, 128, n, 4), np.uint8)
    nib[..., 0::2] = words & 0xF
    nib[..., 1::2] = words >> 4
    vals = E2M1[nib] * np.repeat(np.exp2(scales.astype(np.float64) - 127.0), 8, axis=1)[..., None]
    return vals.transpose(0, 1, 3, 2).reshape(g * 512, n)


def sigmoid(v):
    return 1.0 / (1.0 + np.exp(-np.maximum(v, -700.0)))

def planes(y):
    n, m = y.shape
    v = y.astype(np.float32).astype(ml_dtypes.bfloat16).astype(np.float64).reshape(n // 32, 32, m)
    top = np.abs(v).max(1)
    byte = np.clip(np.where(top > 0, np.frexp(top)[1] - 1 + 127 - 7, 1), 1, 254)
    codes = (v * np.exp2(127.0 - byte)[:, None, :]).reshape(n, m).astype(np.float32).astype(ml_dtypes.float8_e4m3fn).view(np.uint8)
    words = codes.reshape(n // 512, 128, 4, m).transpose(0, 1, 3, 2)
    return np.ascontiguousarray(words), np.ascontiguousarray(byte.astype(np.uint8).reshape(n // 512, 16, m))


K, T, S, V, N, H = 512, 2048, 512, 512, 512, 512


def setup_inputs():
    n = np.random.standard_normal
    s = mx_kscale(K)[:, None]
    u = mx_kscale(S)
    packed_xT = pack_weight(n((K, T)) * s)
    packed_w1 = pack_fp4(n((K, H)) / np.sqrt(K) / s)
    packed_w2 = pack_fp4(n((K, H)) / np.sqrt(K) / s)
    packed_w3 = pack_fp4(n((K, N)) / np.sqrt(K) / s)
    return {
        "x_words": packed_xT[0],
        "x_scales": packed_xT[1],
        "w1_words": packed_w1[0],
        "w1_scales": packed_w1[1],
        "w2_words": packed_w2[0],
        "w2_scales": packed_w2[1],
        "gk": (np.random.uniform(0.5, 1.5, (H, 1)) * u[:, None]).astype(np.float32),
        "gq": (np.random.uniform(0.5, 1.5, (H, 1)) / u[:, None]).astype(np.float32),
        "wv": (n((K, N)) / np.sqrt(K) / s).astype(np.float32),
        "gi": (np.random.uniform(0.5, 1.5, (S, 1)) / u[:, None]).astype(np.float32),
        "w3_words": packed_w3[0],
        "w3_scales": packed_w3[1],
        "res": (0.5 * n((N, V))).astype(np.float32),
        "gt": (np.random.uniform(0.5, 1.5, (S, 1)) * u[:, None]).astype(np.float32),
        "offs": striped(np.random.permutation(T)[:S]),
        "qs": striped(np.random.permutation(T)[:V]),
    }


def reference(x_words, x_scales, w1_words, w1_scales, w2_words, w2_scales, gk, gq, wv, gi, w3_words, w3_scales, res, gt, offs, qs):
    xq = unpack_weight(x_words, x_scales)[:, unstriped(offs)]
    val = xq.T @ mxq(f64(wv), 0, "e4m3")
    zv = f64(gi) * val
    kf = unpack_fp4(w1_words, w1_scales).T @ xq
    z = f64(gk) * kf
    x_qs = unpack_weight(x_words, x_scales)[:, unstriped(qs)]
    qf = unpack_fp4(w2_words, w2_scales).T @ x_qs
    z2 = f64(gq) * qf
    s = 0.0625 * ((mxq(z, 0, "e4m3").T @ mxq(z2, 0, "e4m3")))
    zp = f64(gt) * sigmoid(s)
    og = sigmoid(unpack_fp4(w3_words, w3_scales).T @ x_qs)
    out_0 = f64(res) + (0.0625 * ((mxq(zv, 0, "e4m3").T @ mxq(zp, 0, "e4m3")))) * og
    return (out_0,) + planes(out_0)

@@ -1,0 +1,283 @@
+from contextlib import ExitStack
+
+import concourse.mybir as mybir
+from concourse.masks import make_identity
+
+K, T, S, V, N, H = 512, 2048, 512, 512, 512, 512
+FLOPS = 6 * 2 * 512 * 512 * 512
+
+F32 = mybir.dt.float32
+BF16 = mybir.dt.bfloat16
+I32 = mybir.dt.int32
+U32 = mybir.dt.uint32
+U16 = mybir.dt.uint16
+U8 = mybir.dt.uint8
+FP8X4 = mybir.dt.float8_e4m3fn_x4
+FP4X4 = mybir.dt.float4_e2m1fn_x4
+ACT = mybir.ActivationFunctionType
+ALU = mybir.AluOpType
+
+P = 128
+PACK = 4
+W = 512
+CH = 128
+HALF = 256
+SIXTEENTH = 0.0625
+
+
+def tile_picked_listgate_sigmoid_po_kernel(
+    tc, x_words, x_scales, w1_words, w1_scales, w2_words, w2_scales, gk, gq, wv, gi,
+    w3_words, w3_scales, res, gt, offs, qs, out_0, out_1, out_2,
+):
+    nc = tc.nc
+    with ExitStack() as ctx:
+        keep = ctx.enter_context(tc.tile_pool(name="keep", bufs=1))
+        ring = ctx.enter_context(tc.tile_pool(name="ring", bufs=2))
+        psum = ctx.enter_context(tc.psum_pool(name="psum", bufs=1))
+
+        def sb(name, shape, dtype):
+            return keep.tile(shape, dtype, name=name, align_bytes=64)
+
+        def bank(i):
+            return psum.tile([P, W], F32, name="bank%d" % i, tag="bank%d" % i)
+
+        def load_scales(queue, name, scales, width):
+            plane = sb(name, [P, width], U8)
+            rows = scales[0].bitcast(I32)
+            for q in range(4):
+                queue.dma_start(
+                    out=plane[32 * q : 32 * q + 32, :].bitcast(I32),
+                    in_=rows[4 * q : 4 * q + 4, :].unsqueeze(0).to_broadcast([8, 4, width // 4]),
+                )
+            return plane
+
+        def load_words(queue, name, words, nbytes):
+            tile = sb(name, [P, nbytes], U8)
+            queue.dma_start(out=tile[:].bitcast(I32), in_=words.bitcast(I32))
+            return tile
+
+        warm = sb("warm", [P, 1], F32)
+        nc.vector.memset(warm[:], 0.0)
+        warm2 = sb("warm2", [P, 1], F32)
+        nc.scalar.activation(out=warm2[:], in_=warm[:], func=ACT.Sigmoid)
+        offs_sb = sb("offs_sb", [P, S // 16], U16)
+        nc.sync.dma_start(offs_sb[:], offs)
+        xs = load_scales(nc.sync, "xs", x_scales, T)
+        qs_sb = sb("qs_sb", [P, V // 16], U16)
+        nc.sync.dma_start(qs_sb[:], qs)
+        w1w = load_words(nc.sync, "w1w", w1_words[0], 2 * H)
+        xw = load_words(nc.sync, "xw", x_words[0].rearrange("p c r -> p (c r)"), 4 * T)
+        w1s = load_scales(nc.sync, "w1s", w1_scales, H)
+        w2w = load_words(nc.sync, "w2w", w2_words[0], 2 * H)
+        wv_raw = sb("wv_raw", [P, PACK, N], F32)
+        nc.sync.dma_start(out=wv_raw[:], in_=wv.rearrange("(p j) n -> p j n", j=PACK))
+        w3w = load_words(nc.sync, "w3w", w3_words[0], 2 * N)
+        w2s = load_scales(nc.sync, "w2s", w2_scales, H)
+        res_sb = sb("res_sb", [P, PACK, V], F32)
+        nc.sync.dma_start(out=res_sb[:], in_=res.rearrange("(p t) v -> p t v", t=PACK))
+        w3s = load_scales(nc.sync, "w3s", w3_scales, N)
+        g_rows = sb("g_rows", [P, P], F32)
+        nc.vector.memset(g_rows[:], 0.0)
+        for i, vec in enumerate((gk, gq, gi, gt)):
+            nc.gpsimd.dma_start(
+                out=g_rows[32 * i : 32 * i + PACK, :],
+                in_=vec.rearrange("(b t r) o -> t b (r o)", t=4, r=8),
+            )
+        ident = sb("ident", [P, P], F32)
+        make_identity(nc, ident[:])
+        g_ps = bank(7)
+        nc.tensor.transpose(g_ps[:, 0:P], g_rows[:], ident[:])
+        g_all = sb("g_all", [P, 4 * PACK], F32)
+        nc.scalar.copy(
+            out=g_all[:].rearrange("p (i t) -> p i t", t=PACK),
+            in_=g_ps[:, 0:P].rearrange("p (i u) -> p i u", i=4)[:, :, 0:PACK],
+        )
+        gk_sb, gq_sb, gi_sb, gt_sb = [g_all[:, PACK * i : PACK * (i + 1)] for i in range(4)]
+
+        ks_raw = sb("ks_raw", [P, S], U8)
+        nc.vector.tensor_copy(ks_raw[:], xs[:].indirect(offs_sb[:]))
+        qsc = sb("qsc", [P, V], U8)
+        nc.vector.tensor_copy(qsc[:], xs[:].indirect(qs_sb[:]))
+
+        def deal_runs(name, src, nbytes):
+            dst = sb(name, [P, nbytes], U8)
+            nc.vector.tensor_copy(
+                out=dst[:].bitcast(I32).rearrange("p (t b r) -> p t b r", t=4, b=16),
+                in_=src[:].bitcast(I32).rearrange("p (b t r) -> p t b r", t=4, b=16),
+            )
+            return dst
+
+
+        kw = sb("kw", [P, S], U32)
+        nc.vector.tensor_copy(
+            kw[:].rearrange("p (t b r) -> p b t r", t=4, b=16), xw[:].bitcast(U32).indirect(offs_sb[:])
+        )
+        ksc = deal_runs("ksc", ks_raw, S)
+        w1wd = deal_runs("w1wd", w1w, 2 * H)
+        w1sd = deal_runs("w1sd", w1s, H)
+        qw = sb("qw", [P, V], U32)
+        nc.vector.tensor_copy(qw[:], xw[:].bitcast(U32).indirect(qs_sb[:]))
+        w2wd = deal_runs("w2wd", w2w, 2 * H)
+        w2sd = deal_runs("w2sd", w2s, H)
+        wv_bf = sb("wv_bf", [P, N, PACK], BF16)
+        nc.vector.tensor_copy(
+            out=wv_bf[:].rearrange("p (c i) j -> p c j i", i=4),
+            in_=wv_raw[:].rearrange("p j (c i) -> p c j i", i=4),
+        )
+        w3wd = sb("w3wd", [P, 2 * N], U8)
+        nc.vector.tensor_copy(
+            out=w3wd[:].rearrange("p (t m e) -> p t m e", t=4, e=2),
+            in_=w3w[:].rearrange("p (m t e) -> p t m e", t=4, e=2),
+        )
+
+        def quantise(codes, scales, values):
+            nc.vector.quantize_mx(out=codes.bitcast(FP8X4), scales=scales, in_=values)
+
+        wv_w = sb("wv_w", [P, N], U32)
+        wv_s = sb("wv_s", [P, N], U8)
+        quantise(wv_w[:], wv_s[:], wv_bf[:].rearrange("p n j -> p (n j)"))
+
+        def mm(out, lhs, lhs_s, rhs, rhs_s):
+            nc.tensor.matmul_mx(out=out, lhsT=lhs, lhsT_scale=lhs_s, rhs=rhs, rhs_scale=rhs_s, start=True, stop=True)
+
+        def fp4(words, t):
+            return words[:, 2 * P * t : 2 * P * (t + 1)].bitcast(FP4X4)
+
+        def fp8(words, lo, hi):
+            return words[:, lo:hi].bitcast(FP8X4)
+
+        def weigh(name, banks, weights, view):
+            planes = [sb("%s_h%d" % (name, h), [P, PACK, HALF], BF16) for h in range(2)]
+            for h in range(2):
+                for t in range(PACK):
+                    o, i = view(planes[h][:, t, :], banks[t], h)
+                    nc.scalar.activation(out=o, in_=i, func=ACT.Copy, scale=weights[:, t : t + 1])
+            return planes
+
+        def weave(name, plane):
+            woven = sb(name, [P, HALF, PACK], BF16)
+            nc.vector.tensor_copy(
+                out=woven[:].rearrange("p (c i) t -> p c t i", i=4),
+                in_=plane[:].rearrange("p t (c i) -> p c t i", i=4),
+            )
+            return woven[:].rearrange("p c t -> p (c t)")
+
+        def plain(o, b, h):
+            return o, b[:, h * HALF : (h + 1) * HALF]
+
+        def dealt(o, b, h):
+            return (
+                o.rearrange("p (u m) -> p u m", u=2),
+                b[:].rearrange("p (m u) -> p u m", u=4)[:, 2 * h : 2 * h + 2, :],
+            )
+
+        kf = [bank(t) for t in range(PACK)]
+        for t in range(PACK):
+            mm(kf[t][:], fp4(w1wd, t), w1sd[:, P * t : P * (t + 1)], fp8(kw, 0, S), ksc[:])
+        qf = [bank(4 + t) for t in range(PACK)]
+        for t in range(PACK):
+            mm(qf[t][:], fp4(w2wd, t), w2sd[:, P * t : P * (t + 1)], fp8(qw, 0, V), qsc[:])
+        z_pl = weigh("z", kf, gk_sb, plain)
+        val = [bank(t) for t in range(PACK)]
+        for t in range(PACK):
+            mm(val[t][:], fp8(kw, P * t, P * (t + 1)), ksc[:, P * t : P * (t + 1)], fp8(wv_w, 0, N), wv_s[:])
+        z2_pl = weigh("z2", qf, gq_sb, plain)
+        zv_pl = weigh("zv", val, gi_sb, dealt)
+
+        def weave_and_quantise(name, planes):
+            codes = sb(name + "_w", [P, W], U32)
+            scales = sb(name + "_s", [P, W], U8)
+            woven = [weave("%s_wov%d" % (name, h), planes[h]) for h in range(2)]
+            for h in range(2):
+                cols = slice(h * HALF, (h + 1) * HALF)
+                quantise(codes[:, cols], scales[:, cols], woven[h])
+            return codes, scales
+
+        z_w, z_s = weave_and_quantise("z", z_pl)
+        w3sd = sb("w3sd", [P, N], U8)
+        nc.vector.tensor_copy(
+            out=w3sd[:].rearrange("p (t m) -> p t m", t=4),
+            in_=w3s[:].rearrange("p (m t) -> p t m", t=4),
+        )
+        z2_w, z2_s = weave_and_quantise("z2", z2_pl)
+        zv_w, zv_s = weave_and_quantise("zv", zv_pl)
+
+        zp_w = sb("zp_w", [P, V], U32)
+        zp_s = sb("zp_s", [P, V], U8)
+        y_w = sb("y_w", [P, V], U32)
+        y_s = sb("y_s", [P, V], U8)
+        out_rows = out_0.rearrange("(p t) v -> p t v", t=PACK)
+        out_words = out_1[0].rearrange("p c r -> p (c r)").bitcast(I32)
+        gt_b = gt_sb.unsqueeze(1).to_broadcast([P, CH, PACK])
+        gates = {}
+        ys = {}
+
+        def scores(c):
+            cols = slice(c * CH, (c + 1) * CH)
+            sc = bank(4 + c)
+            for t in range(PACK):
+                mm(sc[:, t * CH : (t + 1) * CH], fp8(z_w, P * t, P * (t + 1)), z_s[:, P * t : P * (t + 1)],
+                   fp8(z2_w, c * CH, (c + 1) * CH), z2_s[:, cols])
+            sig = ring.tile([P, CH, PACK], F32, name="sig")
+            nc.scalar.activation(out=sig[:], in_=sc[:].rearrange("p (t v) -> p v t", t=PACK), func=ACT.Sigmoid, scale=SIXTEENTH)
+            zp = ring.tile([P, CH, PACK], BF16, name="zp", align_bytes=64)
+            nc.vector.tensor_tensor(out=zp[:], in0=sig[:], in1=gt_b, op=ALU.mult)
+            return zp
+
+        def gate(c):
+            cols = slice(c * CH, (c + 1) * CH)
+            og = bank(c)
+            for t in range(PACK):
+                mm(og[:, t * CH : (t + 1) * CH], fp4(w3wd, t), w3sd[:, P * t : P * (t + 1)],
+                   fp8(qw, c * CH, (c + 1) * CH), qsc[:, cols])
+            g = sb("og%d" % c, [P, W], F32)
+            nc.scalar.activation(out=g[:], in_=og[:], func=ACT.Sigmoid)
+            gates[c] = g
+
+        def quantise_zp(c, zp):
+            cols = slice(c * CH, (c + 1) * CH)
+            quantise(zp_w[:, cols], zp_s[:, cols], zp[:].rearrange("p v t -> p (v t)"))
+
+        def product(c):
+            cols = slice(c * CH, (c + 1) * CH)
+            acc = bank(4 + c)
+            for t in range(PACK):
+                mm(acc[:, t * CH : (t + 1) * CH], fp8(zv_w, P * t, P * (t + 1)), zv_s[:, P * t : P * (t + 1)],
+                   fp8(zp_w, c * CH, (c + 1) * CH), zp_s[:, cols])
+            gated = ring.tile([P, W], F32, name="gated")
+            nc.vector.scalar_tensor_tensor(out=gated[:], in0=acc[:], scalar=SIXTEENTH, in1=gates[c][:], op0=ALU.mult, op1=ALU.mult)
+            return gated
+
+        def finish(c, gated):
+            cols = slice(c * CH, (c + 1) * CH)
+            y = sb("y%d" % c, [P, PACK, CH], F32)
+            nc.vector.tensor_tensor(out=y[:], in0=gated[:].rearrange("p (t v) -> p t v", t=PACK), in1=res_sb[:, :, cols], op=ALU.add)
+            nc.sync.dma_start(out=out_rows[:, :, cols], in_=y[:])
+            y_bf = sb("ybf%d" % c, [P, CH, PACK], BF16)
+            nc.scalar.copy(out=y_bf[:], in_=y[:].rearrange("p t v -> p v t"))
+            ys[c] = y_bf
+
+        def hand_on(c):
+            cols = slice(c * CH, (c + 1) * CH)
+            quantise(y_w[:, cols], y_s[:, cols], ys[c][:].rearrange("p v t -> p (v t)"))
+            nc.sync.dma_start(out=out_words[:, cols], in_=y_w[:, cols].bitcast(I32))
+
+        chunks = V // CH
+        zps = {}
+        gated = {}
+        for step in range(chunks + 3):
+            if step < chunks:
+                zps[step] = scores(step)
+                gate(step)
+            if 0 <= step - 2 < chunks:
+                gated[step - 2] = product(step - 2)
+            if 0 <= step - 1 < chunks:
+                quantise_zp(step - 1, zps[step - 1])
+            if 0 <= step - 3 < chunks:
+                hand_on(step - 3)
+            if 0 <= step - 2 < chunks:
+                finish(step - 2, gated[step - 2])
+        out_scale_rows = out_2[0].bitcast(I32)
+        for q in range(4):
+            queue = nc.sync if q % 2 == 0 else nc.scalar
+            queue.dma_start(out=out_scale_rows[4 * q : 4 * q + 4, :], in_=y_s[32 * q : 32 * q + 4, :].bitcast(I32))

@@ -32,24 +32,32 @@ def tile_picked_listgate_sigmoid_po_kernel(
     nc = tc.nc
     with ExitStack() as ctx:
         keep = ctx.enter_context(tc.tile_pool(name="keep", bufs=1))
-        ring = ctx.enter_context(tc.tile_pool(name="ring", bufs=2))
+        ring = ctx.enter_context(tc.tile_pool(name="ring", bufs=4))
         psum = ctx.enter_context(tc.psum_pool(name="psum", bufs=1))
 
-        def sb(name, shape, dtype):
-            return keep.tile(shape, dtype, name=name, align_bytes=64)
+        def sb(name, shape, dtype, tag=None):
+            return keep.tile(shape, dtype, name=name, tag=tag or name, align_bytes=64)
 
         def bank(i):
             return psum.tile([P, W], F32, name="bank%d" % i, tag="bank%d" % i)
 
-        def load_scales(queue, name, scales, width):
+        def load_scale_rows(queue, name, scales, width):
             plane = sb(name, [P, width], U8)
+            nc.gpsimd.memset(plane[:].bitcast(I32), 0)
             rows = scales[0].bitcast(I32)
             for q in range(4):
-                queue.dma_start(
-                    out=plane[32 * q : 32 * q + 32, :].bitcast(I32),
-                    in_=rows[4 * q : 4 * q + 4, :].unsqueeze(0).to_broadcast([8, 4, width // 4]),
-                )
+                queue.dma_start(out=plane[32 * q : 32 * q + 4, :].bitcast(I32), in_=rows[4 * q : 4 * q + 4, :])
             return plane
+
+        def load_weights(queue, name, first, second):
+            rows = sb(name, [P, P], F32)
+            nc.gpsimd.memset(rows[:], 0.0)
+            for i, vec in enumerate((first, second)):
+                queue.dma_start(
+                    out=rows[PACK * i : PACK * (i + 1), :],
+                    in_=vec.rearrange("(b t r) o -> t b (r o)", t=4, r=8),
+                )
+            return rows
 
         def load_words(queue, name, words, nbytes):
             tile = sb(name, [P, nbytes], U8)
@@ -62,37 +70,33 @@ def tile_picked_listgate_sigmoid_po_kernel(
         nc.scalar.activation(out=warm2[:], in_=warm[:], func=ACT.Sigmoid)
         offs_sb = sb("offs_sb", [P, S // 16], U16)
         nc.sync.dma_start(offs_sb[:], offs)
-        xs = load_scales(nc.sync, "xs", x_scales, T)
+        xs = load_scale_rows(nc.sync, "xs", x_scales, T)
         qs_sb = sb("qs_sb", [P, V // 16], U16)
         nc.sync.dma_start(qs_sb[:], qs)
         w1w = load_words(nc.sync, "w1w", w1_words[0], 2 * H)
         xw = load_words(nc.sync, "xw", x_words[0].rearrange("p c r -> p (c r)"), 4 * T)
-        w1s = load_scales(nc.sync, "w1s", w1_scales, H)
-        w2w = load_words(nc.sync, "w2w", w2_words[0], 2 * H)
+        w1s = load_scale_rows(nc.sync, "w1s", w1_scales, H)
+        feature_rows = load_weights(nc.sync, "feature_rows", gk, gq)
         wv_raw = sb("wv_raw", [P, PACK, N], F32)
         nc.sync.dma_start(out=wv_raw[:], in_=wv.rearrange("(p j) n -> p j n", j=PACK))
+        w2w = load_words(nc.sync, "w2w", w2_words[0], 2 * H)
+        w2s = load_scale_rows(nc.sync, "w2s", w2_scales, H)
+        token_rows = load_weights(nc.sync, "token_rows", gi, gt)
         w3w = load_words(nc.sync, "w3w", w3_words[0], 2 * N)
-        w2s = load_scales(nc.sync, "w2s", w2_scales, H)
         res_sb = sb("res_sb", [P, PACK, V], F32)
         nc.sync.dma_start(out=res_sb[:], in_=res.rearrange("(p t) v -> p t v", t=PACK))
-        w3s = load_scales(nc.sync, "w3s", w3_scales, N)
-        g_rows = sb("g_rows", [P, P], F32)
-        nc.vector.memset(g_rows[:], 0.0)
-        for i, vec in enumerate((gk, gq, gi, gt)):
-            nc.gpsimd.dma_start(
-                out=g_rows[32 * i : 32 * i + PACK, :],
-                in_=vec.rearrange("(b t r) o -> t b (r o)", t=4, r=8),
-            )
         ident = sb("ident", [P, P], F32)
         make_identity(nc, ident[:])
-        g_ps = bank(7)
-        nc.tensor.transpose(g_ps[:, 0:P], g_rows[:], ident[:])
-        g_all = sb("g_all", [P, 4 * PACK], F32)
-        nc.scalar.copy(
-            out=g_all[:].rearrange("p (i t) -> p i t", t=PACK),
-            in_=g_ps[:, 0:P].rearrange("p (i u) -> p i u", i=4)[:, :, 0:PACK],
-        )
-        gk_sb, gq_sb, gi_sb, gt_sb = [g_all[:, PACK * i : PACK * (i + 1)] for i in range(4)]
+        w3s = load_scale_rows(nc.sync, "w3s", w3_scales, N)
+
+        def turn_weights(name, rows, bank_number):
+            turned = bank(bank_number)
+            nc.tensor.transpose(turned[:, 0:P], rows[:], ident[:])
+            cols = sb(name, [P, 2 * PACK], F32)
+            nc.scalar.copy(out=cols[:], in_=turned[:, 0 : 2 * PACK])
+            return cols[:, 0:PACK], cols[:, PACK : 2 * PACK]
+
+        gk_sb, gq_sb = turn_weights("feature_cols", feature_rows, 7)
 
         ks_raw = sb("ks_raw", [P, S], U8)
         nc.vector.tensor_copy(ks_raw[:], xs[:].indirect(offs_sb[:]))
@@ -115,19 +119,14 @@ def tile_picked_listgate_sigmoid_po_kernel(
         ksc = deal_runs("ksc", ks_raw, S)
         w1wd = deal_runs("w1wd", w1w, 2 * H)
         w1sd = deal_runs("w1sd", w1s, H)
-        qw = sb("qw", [P, V], U32)
+        qw = sb("qw", [P, V], U32, tag="w1s")
         nc.vector.tensor_copy(qw[:], xw[:].bitcast(U32).indirect(qs_sb[:]))
         w2wd = deal_runs("w2wd", w2w, 2 * H)
         w2sd = deal_runs("w2sd", w2s, H)
-        wv_bf = sb("wv_bf", [P, N, PACK], BF16)
+        wv_bf = sb("wv_bf", [P, N, PACK], BF16, tag="w2s")
         nc.vector.tensor_copy(
             out=wv_bf[:].rearrange("p (c i) j -> p c j i", i=4),
             in_=wv_raw[:].rearrange("p j (c i) -> p c j i", i=4),
-        )
-        w3wd = sb("w3wd", [P, 2 * N], U8)
-        nc.vector.tensor_copy(
-            out=w3wd[:].rearrange("p (t m e) -> p t m e", t=4, e=2),
-            in_=w3w[:].rearrange("p (m t e) -> p t m e", t=4, e=2),
         )
 
         def quantise(codes, scales, values):
@@ -154,13 +153,11 @@ def tile_picked_listgate_sigmoid_po_kernel(
                     nc.scalar.activation(out=o, in_=i, func=ACT.Copy, scale=weights[:, t : t + 1])
             return planes
 
-        def weave(name, plane):
-            woven = sb(name, [P, HALF, PACK], BF16)
-            nc.vector.tensor_copy(
-                out=woven[:].rearrange("p (c i) t -> p c t i", i=4),
+        def weave(copy, woven, plane):
+            copy(
+                out=woven.rearrange("p (c i) t -> p c t i", i=4),
                 in_=plane[:].rearrange("p t (c i) -> p c t i", i=4),
             )
-            return woven[:].rearrange("p c t -> p (c t)")
 
         def plain(o, b, h):
             return o, b[:, h * HALF : (h + 1) * HALF]
@@ -178,29 +175,39 @@ def tile_picked_listgate_sigmoid_po_kernel(
         for t in range(PACK):
             mm(qf[t][:], fp4(w2wd, t), w2sd[:, P * t : P * (t + 1)], fp8(qw, 0, V), qsc[:])
         z_pl = weigh("z", kf, gk_sb, plain)
+        gi_sb, gt_sb = turn_weights("token_cols", token_rows, 3)
         val = [bank(t) for t in range(PACK)]
         for t in range(PACK):
             mm(val[t][:], fp8(kw, P * t, P * (t + 1)), ksc[:, P * t : P * (t + 1)], fp8(wv_w, 0, N), wv_s[:])
         z2_pl = weigh("z2", qf, gq_sb, plain)
         zv_pl = weigh("zv", val, gi_sb, dealt)
 
-        def weave_and_quantise(name, planes):
+        def weave_and_quantise(name, planes, pieces, copies, reuse=None):
             codes = sb(name + "_w", [P, W], U32)
             scales = sb(name + "_s", [P, W], U8)
-            woven = [weave("%s_wov%d" % (name, h), planes[h]) for h in range(2)]
+            woven = sb(name + "_woven", [P, W, PACK], BF16, tag=reuse)
             for h in range(2):
-                cols = slice(h * HALF, (h + 1) * HALF)
-                quantise(codes[:, cols], scales[:, cols], woven[h])
+                weave(copies[h], woven[:, h * HALF : (h + 1) * HALF, :], planes[h])
+            for h in range(pieces):
+                cols = slice(h * W // pieces, (h + 1) * W // pieces)
+                quantise(codes[:, cols], scales[:, cols], woven[:, cols, :].rearrange("p c t -> p (c t)"))
             return codes, scales
 
-        z_w, z_s = weave_and_quantise("z", z_pl)
+        on_vector = (nc.vector.tensor_copy, nc.vector.tensor_copy)
+        shared = (nc.vector.tensor_copy, nc.scalar.copy)
+        z_w, z_s = weave_and_quantise("z", z_pl, 1, on_vector, "w2s")
+        z2_w, z2_s = weave_and_quantise("z2", z2_pl, 2, on_vector)
+        w3wd = sb("w3wd", [P, 2 * N], U8)
+        nc.vector.tensor_copy(
+            out=w3wd[:].rearrange("p (t m e) -> p t m e", t=4, e=2),
+            in_=w3w[:].rearrange("p (m t e) -> p t m e", t=4, e=2),
+        )
         w3sd = sb("w3sd", [P, N], U8)
         nc.vector.tensor_copy(
             out=w3sd[:].rearrange("p (t m) -> p t m", t=4),
             in_=w3s[:].rearrange("p (m t) -> p t m", t=4),
         )
-        z2_w, z2_s = weave_and_quantise("z2", z2_pl)
-        zv_w, zv_s = weave_and_quantise("zv", zv_pl)
+        zv_w, zv_s = weave_and_quantise("zv", zv_pl, 1, shared)
 
         zp_w = sb("zp_w", [P, V], U32)
         zp_s = sb("zp_s", [P, V], U8)
@@ -214,19 +221,19 @@ def tile_picked_listgate_sigmoid_po_kernel(
 
         def scores(c):
             cols = slice(c * CH, (c + 1) * CH)
-            sc = bank(4 + c)
+            sc = bank(c)
             for t in range(PACK):
                 mm(sc[:, t * CH : (t + 1) * CH], fp8(z_w, P * t, P * (t + 1)), z_s[:, P * t : P * (t + 1)],
                    fp8(z2_w, c * CH, (c + 1) * CH), z2_s[:, cols])
             sig = ring.tile([P, CH, PACK], F32, name="sig")
             nc.scalar.activation(out=sig[:], in_=sc[:].rearrange("p (t v) -> p v t", t=PACK), func=ACT.Sigmoid, scale=SIXTEENTH)
-            zp = ring.tile([P, CH, PACK], BF16, name="zp", align_bytes=64)
+            zp = sb("zp%d" % c, [P, CH, PACK], BF16, tag="zv_h0" if c == 0 else None)
             nc.vector.tensor_tensor(out=zp[:], in0=sig[:], in1=gt_b, op=ALU.mult)
             return zp
 
         def gate(c):
             cols = slice(c * CH, (c + 1) * CH)
-            og = bank(c)
+            og = bank(4 + c)
             for t in range(PACK):
                 mm(og[:, t * CH : (t + 1) * CH], fp4(w3wd, t), w3sd[:, P * t : P * (t + 1)],
                    fp8(qw, c * CH, (c + 1) * CH), qsc[:, cols])
@@ -240,7 +247,7 @@ def tile_picked_listgate_sigmoid_po_kernel(
 
         def product(c):
             cols = slice(c * CH, (c + 1) * CH)
-            acc = bank(4 + c)
+            acc = bank(c)
             for t in range(PACK):
                 mm(acc[:, t * CH : (t + 1) * CH], fp8(zv_w, P * t, P * (t + 1)), zv_s[:, P * t : P * (t + 1)],
                    fp8(zp_w, c * CH, (c + 1) * CH), zp_s[:, cols])
@@ -254,29 +261,36 @@ def tile_picked_listgate_sigmoid_po_kernel(
             nc.vector.tensor_tensor(out=y[:], in0=gated[:].rearrange("p (t v) -> p t v", t=PACK), in1=res_sb[:, :, cols], op=ALU.add)
             nc.sync.dma_start(out=out_rows[:, :, cols], in_=y[:])
             y_bf = sb("ybf%d" % c, [P, CH, PACK], BF16)
-            nc.scalar.copy(out=y_bf[:], in_=y[:].rearrange("p t v -> p v t"))
+            if c < chunks - 1:
+                nc.scalar.copy(out=y_bf[:], in_=y[:].rearrange("p t v -> p v t"))
+            else:
+                nc.vector.tensor_copy(
+                    out=y_bf[:].rearrange("p (c i) t -> p c t i", i=4),
+                    in_=y[:].rearrange("p t (c i) -> p c t i", i=4),
+                )
             ys[c] = y_bf
 
         def hand_on(c):
             cols = slice(c * CH, (c + 1) * CH)
             quantise(y_w[:, cols], y_s[:, cols], ys[c][:].rearrange("p v t -> p (v t)"))
-            nc.sync.dma_start(out=out_words[:, cols], in_=y_w[:, cols].bitcast(I32))
+            if c >= chunks - 2:
+                done = slice(0, cols.stop) if c == chunks - 2 else cols
+                nc.sync.dma_start(out=out_words[:, done], in_=y_w[:, done].bitcast(I32))
 
         chunks = V // CH
-        zps = {}
+        zps = [scores(c) for c in range(chunks)]
+        for c in range(chunks):
+            quantise_zp(c, zps[c])
+        for c in range(chunks):
+            gate(c)
         gated = {}
         for step in range(chunks + 3):
             if step < chunks:
-                zps[step] = scores(step)
-                gate(step)
-            if 0 <= step - 2 < chunks:
-                gated[step - 2] = product(step - 2)
+                gated[step] = product(step)
             if 0 <= step - 1 < chunks:
-                quantise_zp(step - 1, zps[step - 1])
+                finish(step - 1, gated[step - 1])
             if 0 <= step - 3 < chunks:
                 hand_on(step - 3)
-            if 0 <= step - 2 < chunks:
-                finish(step - 2, gated[step - 2])
         out_scale_rows = out_2[0].bitcast(I32)
         for q in range(4):
             queue = nc.sync if q % 2 == 0 else nc.scalar

@@ -41,67 +41,77 @@ def tile_picked_listgate_sigmoid_po_kernel(
         def bank(i):
             return psum.tile([P, W], F32, name="bank%d" % i, tag="bank%d" % i)
 
-        def load_scale_rows(queue, name, scales, width):
-            plane = sb(name, [P, width], U8)
-            nc.gpsimd.memset(plane[:].bitcast(I32), 0)
-            rows = scales[0].bitcast(I32)
-            for q in range(4):
-                queue.dma_start(out=plane[32 * q : 32 * q + 4, :].bitcast(I32), in_=rows[4 * q : 4 * q + 4, :])
+        def cleared(plane):
+            nc.vector.memset(plane[:].bitcast(I32), 0)
             return plane
 
-        def load_weights(queue, name, first, second):
+        def load_scale_rows(plane, scales):
+            rows = scales[0].bitcast(I32)
+            for q in range(4):
+                nc.sync.dma_start(out=plane[32 * q : 32 * q + 4, :].bitcast(I32), in_=rows[4 * q : 4 * q + 4, :])
+
+        def load_weights(name, vectors):
             rows = sb(name, [P, P], F32)
-            nc.gpsimd.memset(rows[:], 0.0)
-            for i, vec in enumerate((first, second)):
-                queue.dma_start(
+            nc.vector.memset(rows[:], 0.0)
+            for i, vec in enumerate(vectors):
+                nc.sync.dma_start(
                     out=rows[PACK * i : PACK * (i + 1), :],
                     in_=vec.rearrange("(b t r) o -> t b (r o)", t=4, r=8),
                 )
             return rows
 
-        def load_words(queue, name, words, nbytes):
+        def load_words(name, words, nbytes):
             tile = sb(name, [P, nbytes], U8)
-            queue.dma_start(out=tile[:].bitcast(I32), in_=words.bitcast(I32))
+            nc.sync.dma_start(out=tile[:].bitcast(I32), in_=words.bitcast(I32))
             return tile
 
+        offs_sb = sb("offs_sb", [P, S // 16], U16)
+        nc.sync.dma_start(offs_sb[:], offs)
+        qs_sb = sb("qs_sb", [P, V // 16], U16)
+        nc.sync.dma_start(qs_sb[:], qs)
+        w3w = load_words("w3w", w3_words[0], 2 * N)
+        xs = sb("xs", [P, T], U8)
+        nc.gpsimd.memset(xs[:].bitcast(I32), 0)
+        load_scale_rows(xs, x_scales)
         warm = sb("warm", [P, 1], F32)
         nc.vector.memset(warm[:], 0.0)
         warm2 = sb("warm2", [P, 1], F32)
         nc.scalar.activation(out=warm2[:], in_=warm[:], func=ACT.Sigmoid)
-        offs_sb = sb("offs_sb", [P, S // 16], U16)
-        nc.sync.dma_start(offs_sb[:], offs)
-        xs = load_scale_rows(nc.sync, "xs", x_scales, T)
-        qs_sb = sb("qs_sb", [P, V // 16], U16)
-        nc.sync.dma_start(qs_sb[:], qs)
-        w1w = load_words(nc.sync, "w1w", w1_words[0], 2 * H)
-        xw = load_words(nc.sync, "xw", x_words[0].rearrange("p c r -> p (c r)"), 4 * T)
-        w1s = load_scale_rows(nc.sync, "w1s", w1_scales, H)
-        feature_rows = load_weights(nc.sync, "feature_rows", gk, gq)
+        xw = load_words("xw", x_words[0].rearrange("p c r -> p (c r)"), 4 * T)
+        w1w = load_words("w1w", w1_words[0], 2 * H)
+        w1s = cleared(sb("w1s", [P, H], U8))
+        load_scale_rows(w1s, w1_scales)
+        early_rows = load_weights("early_rows", [gk])
         wv_raw = sb("wv_raw", [P, PACK, N], F32)
         nc.sync.dma_start(out=wv_raw[:], in_=wv.rearrange("(p j) n -> p j n", j=PACK))
-        w2w = load_words(nc.sync, "w2w", w2_words[0], 2 * H)
-        w2s = load_scale_rows(nc.sync, "w2s", w2_scales, H)
-        token_rows = load_weights(nc.sync, "token_rows", gi, gt)
-        w3w = load_words(nc.sync, "w3w", w3_words[0], 2 * N)
+        w2w = load_words("w2w", w2_words[0], 2 * H)
+        w2s = cleared(sb("w2s", [P, H], U8))
+        load_scale_rows(w2s, w2_scales)
+        middle_rows = load_weights("middle_rows", [gq, gi])
+        late_rows = load_weights("late_rows", [gt])
         res_sb = sb("res_sb", [P, PACK, V], F32)
         nc.sync.dma_start(out=res_sb[:], in_=res.rearrange("(p t) v -> p t v", t=PACK))
+        w3s = cleared(sb("w3s", [P, N], U8))
+        load_scale_rows(w3s, w3_scales)
         ident = sb("ident", [P, P], F32)
         make_identity(nc, ident[:])
-        w3s = load_scale_rows(nc.sync, "w3s", w3_scales, N)
 
-        def turn_weights(name, rows, bank_number):
+        def turn_weights(name, rows, count, bank_number):
             turned = bank(bank_number)
             nc.tensor.transpose(turned[:, 0:P], rows[:], ident[:])
-            cols = sb(name, [P, 2 * PACK], F32)
-            nc.scalar.copy(out=cols[:], in_=turned[:, 0 : 2 * PACK])
-            return cols[:, 0:PACK], cols[:, PACK : 2 * PACK]
+            cols = sb(name, [P, count * PACK], F32)
+            nc.scalar.copy(out=cols[:], in_=turned[:, 0 : count * PACK])
+            return [cols[:, PACK * i : PACK * (i + 1)] for i in range(count)]
 
-        gk_sb, gq_sb = turn_weights("feature_cols", feature_rows, 7)
+        [gk_sb] = turn_weights("early_cols", early_rows, 1, 7)
 
+        w3wd = sb("w3wd", [P, 2 * N], U8)
+        nc.vector.tensor_copy(
+            out=w3wd[:].rearrange("p (t g m e) -> p g t m e", t=4, m=8, e=2),
+            in_=w3w[:].rearrange("p (g m t e) -> p g t m e", t=4, m=8, e=2),
+        )
         ks_raw = sb("ks_raw", [P, S], U8)
         nc.vector.tensor_copy(ks_raw[:], xs[:].indirect(offs_sb[:]))
-        qsc = sb("qsc", [P, V], U8)
-        nc.vector.tensor_copy(qsc[:], xs[:].indirect(qs_sb[:]))
 
         def deal_runs(name, src, nbytes):
             dst = sb(name, [P, nbytes], U8)
@@ -112,11 +122,13 @@ def tile_picked_listgate_sigmoid_po_kernel(
             return dst
 
 
+        ksc = deal_runs("ksc", ks_raw, S)
+        qsc = sb("qsc", [P, V], U8)
+        nc.vector.tensor_copy(qsc[:], xs[:].indirect(qs_sb[:]))
         kw = sb("kw", [P, S], U32)
         nc.vector.tensor_copy(
             kw[:].rearrange("p (t b r) -> p b t r", t=4, b=16), xw[:].bitcast(U32).indirect(offs_sb[:])
         )
-        ksc = deal_runs("ksc", ks_raw, S)
         w1wd = deal_runs("w1wd", w1w, 2 * H)
         w1sd = deal_runs("w1sd", w1s, H)
         qw = sb("qw", [P, V], U32, tag="w1s")
@@ -145,9 +157,10 @@ def tile_picked_listgate_sigmoid_po_kernel(
         def fp8(words, lo, hi):
             return words[:, lo:hi].bitcast(FP8X4)
 
-        def weigh(name, banks, weights, view):
-            planes = [sb("%s_h%d" % (name, h), [P, PACK, HALF], BF16) for h in range(2)]
-            for h in range(2):
+        def weigh(name, banks, weights, view, pieces):
+            width = W // pieces
+            planes = [sb("%s_h%d" % (name, h), [P, PACK, width], BF16) for h in range(pieces)]
+            for h in range(pieces):
                 for t in range(PACK):
                     o, i = view(planes[h][:, t, :], banks[t], h)
                     nc.scalar.activation(out=o, in_=i, func=ACT.Copy, scale=weights[:, t : t + 1])
@@ -160,7 +173,7 @@ def tile_picked_listgate_sigmoid_po_kernel(
             )
 
         def plain(o, b, h):
-            return o, b[:, h * HALF : (h + 1) * HALF]
+            return o, b[:]
 
         def dealt(o, b, h):
             return (
@@ -174,40 +187,35 @@ def tile_picked_listgate_sigmoid_po_kernel(
         qf = [bank(4 + t) for t in range(PACK)]
         for t in range(PACK):
             mm(qf[t][:], fp4(w2wd, t), w2sd[:, P * t : P * (t + 1)], fp8(qw, 0, V), qsc[:])
-        z_pl = weigh("z", kf, gk_sb, plain)
-        gi_sb, gt_sb = turn_weights("token_cols", token_rows, 3)
+        z_pl = weigh("z", kf, gk_sb, plain, 1)
+        gq_sb, gi_sb = turn_weights("middle_cols", middle_rows, 2, 0)
         val = [bank(t) for t in range(PACK)]
         for t in range(PACK):
             mm(val[t][:], fp8(kw, P * t, P * (t + 1)), ksc[:, P * t : P * (t + 1)], fp8(wv_w, 0, N), wv_s[:])
-        z2_pl = weigh("z2", qf, gq_sb, plain)
-        zv_pl = weigh("zv", val, gi_sb, dealt)
+        z2_pl = weigh("z2", qf, gq_sb, plain, 1)
+        [gt_sb] = turn_weights("late_cols", late_rows, 1, 4)
+        zv_pl = weigh("zv", val, gi_sb, dealt, 2)
 
-        def weave_and_quantise(name, planes, pieces, copies, reuse=None):
+        def weave_and_quantise(name, planes, copies, tag=None):
             codes = sb(name + "_w", [P, W], U32)
             scales = sb(name + "_s", [P, W], U8)
-            woven = sb(name + "_woven", [P, W, PACK], BF16, tag=reuse)
-            for h in range(2):
-                weave(copies[h], woven[:, h * HALF : (h + 1) * HALF, :], planes[h])
-            for h in range(pieces):
-                cols = slice(h * W // pieces, (h + 1) * W // pieces)
-                quantise(codes[:, cols], scales[:, cols], woven[:, cols, :].rearrange("p c t -> p (c t)"))
+            woven = sb(name + "_woven", [P, W, PACK], BF16, tag=tag)
+            width = W // len(planes)
+            for h, plane in enumerate(planes):
+                weave(copies[h], woven[:, h * width : (h + 1) * width, :], plane)
+            quantise(codes[:], scales[:], woven[:].rearrange("p c t -> p (c t)"))
             return codes, scales
 
         on_vector = (nc.vector.tensor_copy, nc.vector.tensor_copy)
         shared = (nc.vector.tensor_copy, nc.scalar.copy)
-        z_w, z_s = weave_and_quantise("z", z_pl, 1, on_vector, "w2s")
-        z2_w, z2_s = weave_and_quantise("z2", z2_pl, 2, on_vector)
-        w3wd = sb("w3wd", [P, 2 * N], U8)
-        nc.vector.tensor_copy(
-            out=w3wd[:].rearrange("p (t m e) -> p t m e", t=4, e=2),
-            in_=w3w[:].rearrange("p (m t e) -> p t m e", t=4, e=2),
-        )
+        z_w, z_s = weave_and_quantise("z", z_pl, on_vector, "w2s")
+        z2_w, z2_s = weave_and_quantise("z2", z2_pl, on_vector)
         w3sd = sb("w3sd", [P, N], U8)
         nc.vector.tensor_copy(
-            out=w3sd[:].rearrange("p (t m) -> p t m", t=4),
-            in_=w3s[:].rearrange("p (m t) -> p t m", t=4),
+            out=w3sd[:].rearrange("p (t g m) -> p g t m", t=4, m=16),
+            in_=w3s[:].rearrange("p (g m t) -> p g t m", t=4, m=16),
         )
-        zv_w, zv_s = weave_and_quantise("zv", zv_pl, 1, shared)
+        zv_w, zv_s = weave_and_quantise("zv", zv_pl, shared)
 
         zp_w = sb("zp_w", [P, V], U32)
         zp_s = sb("zp_s", [P, V], U8)
@@ -227,9 +235,7 @@ def tile_picked_listgate_sigmoid_po_kernel(
                    fp8(z2_w, c * CH, (c + 1) * CH), z2_s[:, cols])
             sig = ring.tile([P, CH, PACK], F32, name="sig")
             nc.scalar.activation(out=sig[:], in_=sc[:].rearrange("p (t v) -> p v t", t=PACK), func=ACT.Sigmoid, scale=SIXTEENTH)
-            zp = sb("zp%d" % c, [P, CH, PACK], BF16, tag="zv_h0" if c == 0 else None)
-            nc.vector.tensor_tensor(out=zp[:], in0=sig[:], in1=gt_b, op=ALU.mult)
-            return zp
+            nc.vector.tensor_tensor(out=zps[c // 2][:, c % 2], in0=sig[:], in1=gt_b, op=ALU.mult)
 
         def gate(c):
             cols = slice(c * CH, (c + 1) * CH)
@@ -241,9 +247,9 @@ def tile_picked_listgate_sigmoid_po_kernel(
             nc.scalar.activation(out=g[:], in_=og[:], func=ACT.Sigmoid)
             gates[c] = g
 
-        def quantise_zp(c, zp):
-            cols = slice(c * CH, (c + 1) * CH)
-            quantise(zp_w[:, cols], zp_s[:, cols], zp[:].rearrange("p v t -> p (v t)"))
+        def quantise_zp(h):
+            cols = slice(h * HALF, (h + 1) * HALF)
+            quantise(zp_w[:, cols], zp_s[:, cols], zps[h][:].rearrange("p c v t -> p (c v t)"))
 
         def product(c):
             cols = slice(c * CH, (c + 1) * CH)
@@ -264,10 +270,7 @@ def tile_picked_listgate_sigmoid_po_kernel(
             if c < chunks - 1:
                 nc.scalar.copy(out=y_bf[:], in_=y[:].rearrange("p t v -> p v t"))
             else:
-                nc.vector.tensor_copy(
-                    out=y_bf[:].rearrange("p (c i) t -> p c t i", i=4),
-                    in_=y[:].rearrange("p t (c i) -> p c t i", i=4),
-                )
+                weave(nc.vector.tensor_copy, y_bf[:], y)
             ys[c] = y_bf
 
         def hand_on(c):
@@ -278,19 +281,18 @@ def tile_picked_listgate_sigmoid_po_kernel(
                 nc.sync.dma_start(out=out_words[:, done], in_=y_w[:, done].bitcast(I32))
 
         chunks = V // CH
-        zps = [scores(c) for c in range(chunks)]
+        zps = [sb("zp%d" % h, [P, 2, CH, PACK], BF16, tag="zv_h0" if h == 0 else None) for h in range(2)]
         for c in range(chunks):
-            quantise_zp(c, zps[c])
+            scores(c)
+        for h in range(2):
+            quantise_zp(h)
         for c in range(chunks):
             gate(c)
-        gated = {}
-        for step in range(chunks + 3):
-            if step < chunks:
-                gated[step] = product(step)
-            if 0 <= step - 1 < chunks:
-                finish(step - 1, gated[step - 1])
-            if 0 <= step - 3 < chunks:
-                hand_on(step - 3)
+        gated = [product(c) for c in range(chunks)]
+        for c in range(chunks):
+            finish(c, gated[c])
+        for c in range(chunks):
+            hand_on(c)
         out_scale_rows = out_2[0].bitcast(I32)
         for q in range(4):
             queue = nc.sync if q % 2 == 0 else nc.scalar

@@ -264,7 +264,8 @@ def tile_picked_listgate_sigmoid_po_kernel(
         def finish(c, gated):
             cols = slice(c * CH, (c + 1) * CH)
             y = sb("y%d" % c, [P, PACK, CH], F32)
-            nc.vector.tensor_tensor(out=y[:], in0=gated[:].rearrange("p (t v) -> p t v", t=PACK), in1=res_sb[:, :, cols], op=ALU.add)
+            adder = nc.gpsimd if c == 0 else nc.vector
+            adder.tensor_tensor(out=y[:], in0=gated[:].rearrange("p (t v) -> p t v", t=PACK), in1=res_sb[:, :, cols], op=ALU.add)
             nc.sync.dma_start(out=out_rows[:, :, cols], in_=y[:])
             y_bf = sb("ybf%d" % c, [P, CH, PACK], BF16)
             if c < chunks - 1:
@@ -288,10 +289,16 @@ def tile_picked_listgate_sigmoid_po_kernel(
             quantise_zp(h)
         for c in range(chunks):
             gate(c)
-        gated = [product(c) for c in range(chunks)]
-        for c in range(chunks):
+        gated = [product(0)]
+        finish(0, gated[0])
+        gated.append(product(1))
+        for c in range(1, chunks):
+            if c + 1 < chunks:
+                gated.append(product(c + 1))
+            else:
+                hand_on(0)
             finish(c, gated[c])
-        for c in range(chunks):
+        for c in range(1, chunks):
             hand_on(c)
         out_scale_rows = out_2[0].bitcast(I32)
         for q in range(4):

from contextlib import ExitStack

import concourse.mybir as mybir
from concourse.masks import make_identity

K, T, S, V, N, H = 512, 2048, 512, 512, 512, 512
FLOPS = 6 * 2 * 512 * 512 * 512

F32 = mybir.dt.float32
BF16 = mybir.dt.bfloat16
I32 = mybir.dt.int32
U32 = mybir.dt.uint32
U16 = mybir.dt.uint16
U8 = mybir.dt.uint8
FP8X4 = mybir.dt.float8_e4m3fn_x4
FP4X4 = mybir.dt.float4_e2m1fn_x4
ACT = mybir.ActivationFunctionType
ALU = mybir.AluOpType

P = 128
PACK = 4
W = 512
CH = 128
HALF = 256
SIXTEENTH = 0.0625


def tile_picked_listgate_sigmoid_po_kernel(
    tc, x_words, x_scales, w1_words, w1_scales, w2_words, w2_scales, gk, gq, wv, gi,
    w3_words, w3_scales, res, gt, offs, qs, out_0, out_1, out_2,
):
    nc = tc.nc
    with ExitStack() as ctx:
        keep = ctx.enter_context(tc.tile_pool(name="keep", bufs=1))
        ring = ctx.enter_context(tc.tile_pool(name="ring", bufs=4))
        psum = ctx.enter_context(tc.psum_pool(name="psum", bufs=1))

        def sb(name, shape, dtype, tag=None):
            return keep.tile(shape, dtype, name=name, tag=tag or name, align_bytes=64)

        def bank(i):
            return psum.tile([P, W], F32, name="bank%d" % i, tag="bank%d" % i)

        def cleared(plane):
            nc.vector.memset(plane[:].bitcast(I32), 0)
            return plane

        def load_scale_rows(plane, scales):
            rows = scales[0].bitcast(I32)
            for q in range(4):
                nc.sync.dma_start(out=plane[32 * q : 32 * q + 4, :].bitcast(I32), in_=rows[4 * q : 4 * q + 4, :])

        def load_weights(name, vectors):
            rows = sb(name, [P, P], F32)
            nc.vector.memset(rows[:], 0.0)
            for i, vec in enumerate(vectors):
                nc.sync.dma_start(
                    out=rows[PACK * i : PACK * (i + 1), :],
                    in_=vec.rearrange("(b t r) o -> t b (r o)", t=4, r=8),
                )
            return rows

        def load_words(name, words, nbytes):
            tile = sb(name, [P, nbytes], U8)
            nc.sync.dma_start(out=tile[:].bitcast(I32), in_=words.bitcast(I32))
            return tile

        offs_sb = sb("offs_sb", [P, S // 16], U16)
        nc.sync.dma_start(offs_sb[:], offs)
        qs_sb = sb("qs_sb", [P, V // 16], U16)
        nc.sync.dma_start(qs_sb[:], qs)
        w3w = load_words("w3w", w3_words[0], 2 * N)
        xs = sb("xs", [P, T], U8)
        nc.gpsimd.memset(xs[:].bitcast(I32), 0)
        load_scale_rows(xs, x_scales)
        warm = sb("warm", [P, 1], F32)
        nc.vector.memset(warm[:], 0.0)
        warm2 = sb("warm2", [P, 1], F32)
        nc.scalar.activation(out=warm2[:], in_=warm[:], func=ACT.Sigmoid)
        xw = load_words("xw", x_words[0].rearrange("p c r -> p (c r)"), 4 * T)
        w1w = load_words("w1w", w1_words[0], 2 * H)
        w1s = cleared(sb("w1s", [P, H], U8))
        load_scale_rows(w1s, w1_scales)
        early_rows = load_weights("early_rows", [gk])
        wv_raw = sb("wv_raw", [P, PACK, N], F32)
        nc.sync.dma_start(out=wv_raw[:], in_=wv.rearrange("(p j) n -> p j n", j=PACK))
        w2w = load_words("w2w", w2_words[0], 2 * H)
        w2s = cleared(sb("w2s", [P, H], U8))
        load_scale_rows(w2s, w2_scales)
        middle_rows = load_weights("middle_rows", [gq, gi])
        late_rows = load_weights("late_rows", [gt])
        res_sb = sb("res_sb", [P, PACK, V], F32)
        nc.sync.dma_start(out=res_sb[:], in_=res.rearrange("(p t) v -> p t v", t=PACK))
        w3s = cleared(sb("w3s", [P, N], U8))
        load_scale_rows(w3s, w3_scales)
        ident = sb("ident", [P, P], F32)
        make_identity(nc, ident[:])

        def turn_weights(name, rows, count, bank_number):
            turned = bank(bank_number)
            nc.tensor.transpose(turned[:, 0:P], rows[:], ident[:])
            cols = sb(name, [P, count * PACK], F32)
            nc.scalar.copy(out=cols[:], in_=turned[:, 0 : count * PACK])
            return [cols[:, PACK * i : PACK * (i + 1)] for i in range(count)]

        [gk_sb] = turn_weights("early_cols", early_rows, 1, 7)

        w3wd = sb("w3wd", [P, 2 * N], U8)
        nc.vector.tensor_copy(
            out=w3wd[:].rearrange("p (t g m e) -> p g t m e", t=4, m=8, e=2),
            in_=w3w[:].rearrange("p (g m t e) -> p g t m e", t=4, m=8, e=2),
        )
        ks_raw = sb("ks_raw", [P, S], U8)
        nc.vector.tensor_copy(ks_raw[:], xs[:].indirect(offs_sb[:]))

        def deal_runs(name, src, nbytes):
            dst = sb(name, [P, nbytes], U8)
            nc.vector.tensor_copy(
                out=dst[:].bitcast(I32).rearrange("p (t b r) -> p t b r", t=4, b=16),
                in_=src[:].bitcast(I32).rearrange("p (b t r) -> p t b r", t=4, b=16),
            )
            return dst


        ksc = deal_runs("ksc", ks_raw, S)
        qsc = sb("qsc", [P, V], U8)
        nc.vector.tensor_copy(qsc[:], xs[:].indirect(qs_sb[:]))
        kw = sb("kw", [P, S], U32)
        nc.vector.tensor_copy(
            kw[:].rearrange("p (t b r) -> p b t r", t=4, b=16), xw[:].bitcast(U32).indirect(offs_sb[:])
        )
        w1wd = deal_runs("w1wd", w1w, 2 * H)
        w1sd = deal_runs("w1sd", w1s, H)
        qw = sb("qw", [P, V], U32, tag="w1s")
        nc.vector.tensor_copy(qw[:], xw[:].bitcast(U32).indirect(qs_sb[:]))
        w2wd = deal_runs("w2wd", w2w, 2 * H)
        w2sd = deal_runs("w2sd", w2s, H)
        wv_bf = sb("wv_bf", [P, N, PACK], BF16, tag="w2s")
        nc.vector.tensor_copy(
            out=wv_bf[:].rearrange("p (c i) j -> p c j i", i=4),
            in_=wv_raw[:].rearrange("p j (c i) -> p c j i", i=4),
        )

        def quantise(codes, scales, values):
            nc.vector.quantize_mx(out=codes.bitcast(FP8X4), scales=scales, in_=values)

        wv_w = sb("wv_w", [P, N], U32)
        wv_s = sb("wv_s", [P, N], U8)
        quantise(wv_w[:], wv_s[:], wv_bf[:].rearrange("p n j -> p (n j)"))

        def mm(out, lhs, lhs_s, rhs, rhs_s):
            nc.tensor.matmul_mx(out=out, lhsT=lhs, lhsT_scale=lhs_s, rhs=rhs, rhs_scale=rhs_s, start=True, stop=True)

        def fp4(words, t):
            return words[:, 2 * P * t : 2 * P * (t + 1)].bitcast(FP4X4)

        def fp8(words, lo, hi):
            return words[:, lo:hi].bitcast(FP8X4)

        def weigh(name, banks, weights, view, pieces):
            width = W // pieces
            planes = [sb("%s_h%d" % (name, h), [P, PACK, width], BF16) for h in range(pieces)]
            for h in range(pieces):
                for t in range(PACK):
                    o, i = view(planes[h][:, t, :], banks[t], h)
                    nc.scalar.activation(out=o, in_=i, func=ACT.Copy, scale=weights[:, t : t + 1])
            return planes

        def weave(copy, woven, plane):
            copy(
                out=woven.rearrange("p (c i) t -> p c t i", i=4),
                in_=plane[:].rearrange("p t (c i) -> p c t i", i=4),
            )

        def plain(o, b, h):
            return o, b[:]

        def dealt(o, b, h):
            return (
                o.rearrange("p (u m) -> p u m", u=2),
                b[:].rearrange("p (m u) -> p u m", u=4)[:, 2 * h : 2 * h + 2, :],
            )

        kf = [bank(t) for t in range(PACK)]
        for t in range(PACK):
            mm(kf[t][:], fp4(w1wd, t), w1sd[:, P * t : P * (t + 1)], fp8(kw, 0, S), ksc[:])
        qf = [bank(4 + t) for t in range(PACK)]
        for t in range(PACK):
            mm(qf[t][:], fp4(w2wd, t), w2sd[:, P * t : P * (t + 1)], fp8(qw, 0, V), qsc[:])
        z_pl = weigh("z", kf, gk_sb, plain, 1)
        gq_sb, gi_sb = turn_weights("middle_cols", middle_rows, 2, 0)
        val = [bank(t) for t in range(PACK)]
        for t in range(PACK):
            mm(val[t][:], fp8(kw, P * t, P * (t + 1)), ksc[:, P * t : P * (t + 1)], fp8(wv_w, 0, N), wv_s[:])
        z2_pl = weigh("z2", qf, gq_sb, plain, 1)
        [gt_sb] = turn_weights("late_cols", late_rows, 1, 4)
        zv_pl = weigh("zv", val, gi_sb, dealt, 2)

        def weave_and_quantise(name, planes, copies, tag=None):
            codes = sb(name + "_w", [P, W], U32)
            scales = sb(name + "_s", [P, W], U8)
            woven = sb(name + "_woven", [P, W, PACK], BF16, tag=tag)
            width = W // len(planes)
            for h, plane in enumerate(planes):
                weave(copies[h], woven[:, h * width : (h + 1) * width, :], plane)
            quantise(codes[:], scales[:], woven[:].rearrange("p c t -> p (c t)"))
            return codes, scales

        on_vector = (nc.vector.tensor_copy, nc.vector.tensor_copy)
        shared = (nc.vector.tensor_copy, nc.scalar.copy)
        z_w, z_s = weave_and_quantise("z", z_pl, on_vector, "w2s")
        z2_w, z2_s = weave_and_quantise("z2", z2_pl, on_vector)
        w3sd = sb("w3sd", [P, N], U8)
        nc.vector.tensor_copy(
            out=w3sd[:].rearrange("p (t g m) -> p g t m", t=4, m=16),
            in_=w3s[:].rearrange("p (g m t) -> p g t m", t=4, m=16),
        )
        zv_w, zv_s = weave_and_quantise("zv", zv_pl, shared)

        zp_w = sb("zp_w", [P, V], U32)
        zp_s = sb("zp_s", [P, V], U8)
        y_w = sb("y_w", [P, V], U32)
        y_s = sb("y_s", [P, V], U8)
        out_rows = out_0.rearrange("(p t) v -> p t v", t=PACK)
        out_words = out_1[0].rearrange("p c r -> p (c r)").bitcast(I32)
        gt_b = gt_sb.unsqueeze(1).to_broadcast([P, CH, PACK])
        gates = {}
        ys = {}

        def scores(c):
            cols = slice(c * CH, (c + 1) * CH)
            sc = bank(c)
            for t in range(PACK):
                mm(sc[:, t * CH : (t + 1) * CH], fp8(z_w, P * t, P * (t + 1)), z_s[:, P * t : P * (t + 1)],
                   fp8(z2_w, c * CH, (c + 1) * CH), z2_s[:, cols])
            sig = ring.tile([P, CH, PACK], F32, name="sig")
            nc.scalar.activation(out=sig[:], in_=sc[:].rearrange("p (t v) -> p v t", t=PACK), func=ACT.Sigmoid, scale=SIXTEENTH)
            nc.vector.tensor_tensor(out=zps[c // 2][:, c % 2], in0=sig[:], in1=gt_b, op=ALU.mult)

        def gate(c):
            cols = slice(c * CH, (c + 1) * CH)
            og = bank(4 + c)
            for t in range(PACK):
                mm(og[:, t * CH : (t + 1) * CH], fp4(w3wd, t), w3sd[:, P * t : P * (t + 1)],
                   fp8(qw, c * CH, (c + 1) * CH), qsc[:, cols])
            g = sb("og%d" % c, [P, W], F32)
            nc.scalar.activation(out=g[:], in_=og[:], func=ACT.Sigmoid)
            gates[c] = g

        def quantise_zp(h):
            cols = slice(h * HALF, (h + 1) * HALF)
            quantise(zp_w[:, cols], zp_s[:, cols], zps[h][:].rearrange("p c v t -> p (c v t)"))

        def product(c):
            cols = slice(c * CH, (c + 1) * CH)
            acc = bank(c)
            for t in range(PACK):
                mm(acc[:, t * CH : (t + 1) * CH], fp8(zv_w, P * t, P * (t + 1)), zv_s[:, P * t : P * (t + 1)],
                   fp8(zp_w, c * CH, (c + 1) * CH), zp_s[:, cols])
            gated = ring.tile([P, W], F32, name="gated")
            nc.vector.scalar_tensor_tensor(out=gated[:], in0=acc[:], scalar=SIXTEENTH, in1=gates[c][:], op0=ALU.mult, op1=ALU.mult)
            return gated

        def finish(c, gated):
            cols = slice(c * CH, (c + 1) * CH)
            y = sb("y%d" % c, [P, PACK, CH], F32)
            adder = nc.gpsimd if c == 0 else nc.vector
            adder.tensor_tensor(out=y[:], in0=gated[:].rearrange("p (t v) -> p t v", t=PACK), in1=res_sb[:, :, cols], op=ALU.add)
            nc.sync.dma_start(out=out_rows[:, :, cols], in_=y[:])
            y_bf = sb("ybf%d" % c, [P, CH, PACK], BF16)
            if c < chunks - 1:
                nc.scalar.copy(out=y_bf[:], in_=y[:].rearrange("p t v -> p v t"))
            else:
                weave(nc.vector.tensor_copy, y_bf[:], y)
            ys[c] = y_bf

        def hand_on(c):
            cols = slice(c * CH, (c + 1) * CH)
            quantise(y_w[:, cols], y_s[:, cols], ys[c][:].rearrange("p v t -> p (v t)"))
            if c >= chunks - 2:
                done = slice(0, cols.stop) if c == chunks - 2 else cols
                nc.sync.dma_start(out=out_words[:, done], in_=y_w[:, done].bitcast(I32))

        chunks = V // CH
        zps = [sb("zp%d" % h, [P, 2, CH, PACK], BF16, tag="zv_h0" if h == 0 else None) for h in range(2)]
        for c in range(chunks):
            scores(c)
        for h in range(2):
            quantise_zp(h)
        for c in range(chunks):
            gate(c)
        gated = [product(0)]
        finish(0, gated[0])
        gated.append(product(1))
        for c in range(1, chunks):
            if c + 1 < chunks:
                gated.append(product(c + 1))
            else:
                hand_on(0)
            finish(c, gated[c])
        for c in range(1, chunks):
            hand_on(c)
        out_scale_rows = out_2[0].bitcast(I32)
        for q in range(4):
            queue = nc.sync if q % 2 == 0 else nc.scalar
            queue.dma_start(out=out_scale_rows[4 * q : 4 * q + 4, :], in_=y_s[32 * q : 32 * q + 4, :].bitcast(I32))
